import numpy as np, ml_dtypes
CORES = [16,18,20,22]
N = 4
import mx_ref
BF = ml_dtypes.bfloat16
def gentries(a):
    return np.ascontiguousarray(a.reshape(8, 16, -1).transpose(0, 2, 1)).reshape(8, -1)
def gtable(e):
    e = np.asarray(e); return np.ascontiguousarray(e.reshape(8, -1, 16).transpose(0, 2, 1)).reshape(128, -1).astype(np.int32)
def gcols(t, e):
    v = np.concatenate([t.reshape(8, 16, -1, 4), np.zeros((8, 16, 1, 4), BF)], axis=2)
    return np.ascontiguousarray(np.stack([v[g][:, e[g]] for g in range(8)])).reshape(128, -1)
def tile(rs):
    return np.stack(rs, axis=2).reshape(128, -1).astype(BF)
def pick(q, e):
    c = np.concatenate([q[0].reshape(128, -1, 4), np.zeros((128, 1, 4), np.uint8)], axis=1); s = np.concatenate([q[1], np.ones((16, 1), np.uint8)], axis=1)
    return (np.ascontiguousarray(c[:, e].reshape(128, -1)), np.ascontiguousarray(s[:, e]))
def join(*qs):
    return (np.concatenate([q[0] for q in qs], axis=1), np.concatenate([q[1] for q in qs], axis=1))
def put(q, e, v):
    c, s = q[0].reshape(128, -1, 4).copy(), q[1].copy(); c[:, e] = v[0].reshape(128, -1, 4); s[:, e] = v[1]
    return (c.reshape(128, -1), s)
def pk(c, s):
    return (np.ascontiguousarray(c), mx_ref.live(s))
def emit(q):
    return q[0], q[1]
def packed(v, rng):
    q = [mx_ref.quantize(np.ascontiguousarray(v[r])) for r in range(N)]
    return np.stack([a for a, b in q]), np.stack([mx_ref.plane(b, rng) for a, b in q])
def values_of_codes():
    e, c = np.zeros((128, 128, 4), np.float32), np.zeros((128, 2, 4), np.uint8)
    e[np.arange(128), np.arange(128), 0] = 1
    c[:127, :, 0] = np.arange(256).reshape(2, 128).T[:127]
    return mx_ref.matmul(mx_ref.quantize(e.reshape(128, 512).astype(BF)), (c.reshape(128, 8), np.full((16, 2), 127, np.uint8))).T.reshape(-1).astype(np.float64)
CODE_VALUE, SCALE_VALUE = values_of_codes(), 2.0 ** (np.arange(256) - 127.0)
def decode(q):
    return (CODE_VALUE[q[0]].reshape(16, 8, -1, 4) * SCALE_VALUE[q[1]][:, None, :, None] + 0.0).reshape(128, -1).astype(np.float32)
def f(rng, *shape):
    return mx_ref.flush((rng.standard_normal(shape, dtype=np.float32) * np.exp2(rng.integers(-2, 3, shape[:-1] + (1,)))).astype(BF))
def wide(rng, *shape, cols=0):
    v = rng.standard_normal(shape, dtype=np.float32) * np.exp2(rng.integers(-12, 13, shape)).astype(np.float32)
    if cols: v *= np.repeat(np.exp2(rng.integers(-cols, cols + 1, shape[:-2] + (1, shape[-1] // 4))) * (rng.random(shape[:-2] + (1, shape[-1] // 4)) > 0.0625), 4, axis=-1).astype(np.float32)
    return mx_ref.flush(v.astype(BF))
C, DOUBLINGS = 384, 9
STEP = [1, 2, 3]
def numbers_of(rng):
    return {"x": np.array(f(rng, N, 128, 4 * C)), "u": np.array(f(rng, N, 128, 512)), "v": np.array(f(rng, N, 128, 512))}
def links(rng, far=False):
    l = rng.permuted(np.tile(np.arange(C), (N, 8, 2, 1)), axis=3)
    if far:
        for r in range(N):
            for i, g in enumerate(rng.permutation(8)[:6]):
                o = rng.permutation(C)
                l[r, g, 0, o] = np.append(o[1:], o[[0, C - 1, C // 2][i % 3]])
                if i < 3: l[r, g, 1] = l[r, g, 0]
    return l
def stored(l):
    return {"la": np.stack([gtable(l[r, :, 0]) for r in range(N)]), "lb": np.stack([gtable(l[r, :, 1]) for r in range(N)])}
def layers(rng, still=[]):
    w = np.array(f(rng, N, 128, 2048)).reshape(N, 8, 16, 4, 8, 16, 4)
    for i in still:
        w[:, :, i] = 0
        w[:, :, :, :, :, i] = 0
    return w
def weights(rng, w):
    c, p = packed(np.ascontiguousarray(w).reshape(N, 128, 2048), rng)
    return {"wc": c, "ws": p}
def setup_inputs(rng):
    return {**numbers_of(rng), **stored(links(rng)), **weights(rng, layers(rng))}
def setup_inputs_ties(rng):
    d = numbers_of(rng)
    o = rng.permutation(N)
    k = rng.integers(-2, 3, (N, 8, C))
    k[o[1]] = -rng.integers(1, 5, (8, C))
    far = rng.permutation(8)
    k[o[2], far[:4]] = 1
    k[o[3], rng.permutation(8)[:4]] = -1
    l = links(rng, True)
    way = rng.permutation(C)
    way[-2:] = np.sort(way[-2:])
    for g, end, top in ((far[4], way[-1], way[-1]), (far[5], way[0], 0)):
        l[o[2], g, 0, way] = np.append(way[1:], end)
        l[o[2], g, 1] = np.arange(C)
        k[o[2], g] = 1
        k[o[2], g, top] = 2
    x = d["x"].reshape(N, 8, 16, C, 4)
    x[:, :, 0] = 0
    x[:, :, 0, :, 0] = k.astype(np.float32).astype(BF)
    u = d["u"].reshape(N, 128, 128, 4)
    u[:, :, ::16] = 0
    for r in range(N):
        for h in range(0, 128, 16): u[r, h, h, 0] = 0.0 if r == o[0] else 1.0
    return {"x": x.reshape(N, 128, 4 * C), "u": u.reshape(N, 128, 512), "v": d["v"], **stored(l), **weights(rng, layers(rng, [0]))}
def setup_inputs_near(rng):
    d = numbers_of(rng)
    x = d["x"].astype(np.float32).reshape(N, 8, 16, C, 4)
    x[:, :, 0] = 0
    x[:, :, 8:] = 0
    u = d["u"].reshape(N, 128, 128, 4)
    u[:, :, ::16] = 0
    w = layers(rng, [0, 8, 9, 10, 11, 12, 13, 14, 15])
    o = rng.permutation(N) % 4
    for r in range(N):
        s = rng.integers(0, 16, (8, C))
        digits = ((s[:, :, None] >> np.arange(4)) & 1) * np.exp2(np.arange(4) - 23.0)
        if o[r] < 3: x[r, :, 12, :, 0] = rng.choice([-1.0, 1.0], (8, C)) * 2.0 ** -20
        if o[r] < 2:
            x[r, :, 0, :, 0] = np.where(rng.permutation(8) < 4, -1.0, 1.0)[:, None]
            x[r, :, 8] = digits
            x[r, :, 11, :, 0] = 2.0 ** -10
        elif o[r] == 2: x[r, :, 8] = digits * rng.choice([-1.0, 1.0], (8, C, 1))
        else:
            e = rng.integers(-1, 2, (8, C)) * 2.0 ** -30
            x[r, :, 8, :, 0] = 1.25 * e
            x[r, :, 9, :, 0] = -1.125 * e
            x[r, :, 15, :, 0] = 2.0 ** -30
            for g in range(8):
                w[r, g, 12, 0, g, 10, 0] = 2.0 ** -18
                w[r, g, 14, 0, g, 10, 0] = 2.0 ** -8
        at = [0, C - 1, int(rng.integers(C)), int(rng.integers(C))]
        for g, j in zip(rng.permutation(8)[:4], at): x[r, g, 0, j, 0] = 2.0 ** 29 * rng.choice([-1.0, 1.0])
        k = 1.0 if o[r] == 0 else 2.0 ** -30
        for h in range(0, 128, 16):
            u[r, h, h, 0] = k if o[r] < 2 else 1.0
            if o[r] < 2: u[r, h + 11, h, 0] = k
            if o[r] < 3: u[r, h + 8, h] = k
            else:
                u[r, h + 8, h, 0] = k
                u[r, h + 9, h, 0] = 1.125 * k
                u[r, h + 10, h, 0] = k
    return {"x": x.reshape(N, 128, 4 * C).astype(BF), "u": u.reshape(N, 128, 512), "v": d["v"], **stored(links(rng, True)), **weights(rng, w)}
def setup_inputs_odd(rng):
    d = numbers_of(rng)
    x = (1.0 + (2 * rng.integers(0, 64, (N, 16, 8, C, 4)) + 1) * 2.0 ** -7) * np.exp2(-rng.integers(0, 7, (N, 16, 8, C, 4)).astype(np.float64)) * rng.choice([-1.0, 1.0], (N, 16, 8, C, 4))
    x[:, :, 0, :, 0] = np.where(rng.random((N, 16, C)) < 0.25, 1.875, 1.96875) * 2.0 ** 8
    x[:, ::2, 1, :, 0] = rng.choice([-1.0, 1.0], (N, 8, C)) * (8 + rng.integers(0, 2, (N, 8, C))) * 2.0 ** -8
    u = d["u"].reshape(N, 16, 8, 128, 4)
    u[:, :, :, ::16] = 0
    for g in range(8): u[:, 2 * g, 1, 16 * g, 0] = 1.0
    return {"x": x.astype(np.float32).reshape(N, 128, 4 * C).astype(BF), "u": u.reshape(N, 128, 512), "v": d["v"], **stored(links(rng)), **weights(rng, layers(rng, [0, 8]))}
def setup_inputs_ends(rng):
    d = numbers_of(rng)
    o, e = rng.permutation(N) % 4, rng.permutation(N) % 4
    m = int(rng.integers(8))
    l = links(rng, True)
    small = -(1.0 + 0.125 * rng.integers(0, 8, (N, 8, 16, C, 4)))
    x = -(0.88 + 0.08 * rng.random((N, 8, 16, C, 4))) * 2.0 ** 30
    x[o == 1] *= rng.choice([-1.0, 1.0], (N, 1, 1, C, 1))[o == 1]
    x[o == 2] = small[o == 2] * 2.0 ** -30
    x[o == 3] = d["x"].astype(np.float32).reshape(N, 8, 16, C, 4)[o == 3][:, :, :, :1]
    x[:, m] = small[:, m] * 2.0 ** -20
    u = d["u"].astype(np.float32).reshape(N, 8, 16, 128, 4)
    v = rng.choice([-1.0, 1.0], (N, 128, 512)) * np.where(o < 2, 2.0 ** 30, 2.0 ** -30)[:, None, None]
    w = np.zeros((N, 128, 4, 128, 4), np.float32)
    i = np.arange(128)
    for r in range(N):
        h = rng.permutation(8)
        c = np.where(h < 2, 0.0, h % 2 * 2.0 - 1.0)[:, None]
        if o[r] < 2: u[r, :, :, ::16] = c * (0.9 + 0.1 * rng.random((8, 16, 8, 4))) * 2.0 ** 30
        if o[r] == 2: u[r, :, :, ::16] = c * (1.0 + 0.125 * rng.integers(0, 8, (8, 16, 8, 4))) * 2.0 ** -30
        if o[r] == 3: u[r, :, :, ::16] *= np.abs(c).astype(np.float32)
        k = np.zeros(8)
        if o[r] < 2: k = rng.choice([-1.0, 1.0], 8) * np.array([0.75, 0.5, 2.0 ** -8])[rng.permutation(8) % 3]
        k[m] = 2.0 ** 8
        for b in range(4): w[r, i, b, i, b] = k[i // 16]
        if e[r] < 2:
            l[r, :, e[r]] = C - 1
            l[r, :, 1 - e[r]] = 0
        if e[r] == 2: l[r] = rng.integers(0, C, (8, 2, C))
    u[:, m, :, ::16] = 0
    return {"x": x.astype(np.float32).reshape(N, 128, 4 * C).astype(BF), "u": u.reshape(N, 128, 512).astype(BF), "v": v.astype(np.float32).astype(BF), **stored(l), **weights(rng, w.astype(BF))}
def setup_inputs_spread(rng):
    d = setup_inputs(rng)
    d["x"] = wide(rng, N, 128, 4 * C, cols=6)
    return d
def check_inputs(d):
    b = []
    for k in ("x", "u", "v"):
        a = np.abs(d[k].astype(np.float32))
        if not (np.isfinite(a).all() and ((a == 0) | (a >= 2.0 ** -30) & (a <= 2.0 ** 30)).all()): b.append("a value of " + k)
    for k in ("la", "lb"):
        if not ((d[k] >= 0) & (d[k] < C)).all(): b.append("an entry of " + k)
    none, least, most = [emit(mx_ref.quantize(np.full((128, 16), k, np.float32).astype(BF)))[1][0, 0] for k in (0.0, 2.0 ** -8, 2.0 ** 8)]
    for r in range(N):
        if ((d["wc"][r] == 0x7F) | (d["wc"][r] == 0xFF)).any(): b.append("wc: a code that is no number")
        s = mx_ref.live(d["ws"][r])
        if ((s != none) & ((s < least) | (s > most))).any(): b.append("ws: a scale out of range")
        if (((d["wc"][r].reshape(16, 8, 512, 4) & 0x7F) != 0) & (s == none)[:, None, :, None]).any(): b.append("wc: a code other than zero under the scale of zeros")
    return b
def look(t, e):
    return np.take_along_axis(t, e, axis=1)
def leaders(p):
    low, at = np.tile(np.arange(C), (8, 1)), p
    for k in range(DOUBLINGS):
        low = np.minimum(low, look(low, at))
        at = look(at, at)
    return look(low, at)
def reference(x, u, v, la, lb, wc, ws):
    qu = [mx_ref.quantize(u[r]) for r in range(N)]
    lay = [pk(wc[r], ws[r]) for r in range(N)]
    l0, l1 = [gentries(la[r]) for r in range(N)], [gentries(lb[r]) for r in range(N)]
    now = [x[r] for r in range(N)]
    for step in STEP:
        own, torn, sent = [], [], []
        for r in range(N):
            q = mx_ref.quantize(now[r])
            s = mx_ref.matmul(qu[r], q)[::16] + np.float32(0.0)
            p = np.where(s < 0, l1[r], l0[r])
            lead = leaders(p)
            e = np.where(lead == np.arange(C), lead, p)
            own.append(decode(q).astype(BF))
            torn.append(e)
            z = own[r]
            for k in range(3):
                z = ((z.astype(np.float32) + gcols(z, e).astype(np.float32)) * np.float32(0.5)).astype(BF)
                e = look(e, e)
            sent.append(mx_ref.quantize(z))
            change = look(s, lead) > s
            l0[r], l1[r] = np.where(change, l1[r], l0[r]), np.where(change, l0[r], l1[r])
        for r in range(N):
            z = sent[(r - step) % N]
            h = tile([mx_ref.matmul(pick(lay[r], np.arange(128 * b, 128 * b + 128)), z) * np.float32(0.03125) for b in range(4)])
            now[r] = (own[r].astype(np.float32) + gcols(h, torn[r]).astype(np.float32)).astype(BF)
    y, ls = np.zeros((N, 128, C), np.float32), np.zeros((N, 8, 2 * C), np.float32)
    oc, osc = np.zeros((N, 128, 4 * C), np.uint8), np.zeros((N, 16, C), np.uint8)
    for r in range(N):
        q = mx_ref.quantize(now[r])
        y[r] = mx_ref.matmul(mx_ref.quantize(v[r]), q)
        ls[r] = np.concatenate([l0[r], l1[r]], axis=1)
        oc[r], osc[r] = emit(q)
    return {"y": y, "ls": ls, "oc": oc, "osc": osc}

@@ -1,0 +1,416 @@
+from concourse.bass import DstId, RemoteDMATransfer
+from concourse.mybir import dt, AluOpType, ActivationFunctionType
+
+C = 384
+HALF = C // 2
+STEPS = [1, 2, 3]
+KT = C // 16
+ROWS = 34
+SLOTS = 14
+TABS = 20
+BIG, LIFT, MID = 2048.0, 512.0, 192.0
+
+SCRATCH = {
+    "ut": ("sbuf", [128, 512], "bfloat16"), "qu": ("sbuf", [128, 128], "float8_e4m3fn_x4"), "qus": ("sbuf", [128, 128], "uint8"),
+    "qr": ("sbuf", [128, 128], "float8_e4m3fn_x4"), "qrs": ("sbuf", [128, 128], "uint8"),
+    "vt": ("sbuf", [128, 512], "bfloat16"), "qv": ("sbuf", [128, 128], "float8_e4m3fn_x4"), "qvs": ("sbuf", [128, 128], "uint8"),
+    "wq": ("sbuf", [128, 512], "float8_e4m3fn_x4"), "wp": ("sbuf", [128, 512], "uint8"),
+    "ones": ("sbuf", [128, 528], "bfloat16"), "et": ("sbuf", [128, 528], "bfloat16"),
+    "qe": ("sbuf", [128, 512], "float8_e4m3fn_x4"), "qes": ("sbuf", [128, 512], "uint8"),
+    "lai": ("sbuf", [128, KT], "int32"), "lbi": ("sbuf", [128, KT], "int32"),
+    "im": ("sbuf", [128, C], "int32"), "im2": ("sbuf", [128, C], "int32"), "ma": ("sbuf", [128, C], "float32"), "mb": ("sbuf", [128, C], "bfloat16"),
+    "mask": ("sbuf", [128, C], "bfloat16"), "ik": ("sbuf", [128, KT], "int32"), "ip": ("sbuf", [128, 8], "int32"),
+    "cols": ("sbuf", [128, 16], "float32"), "plist": ("sbuf", [128, 8], "uint16"),
+    "num": ("sbuf", [128, C], "float32"), "lsr": ("sbuf", [128, 2 * C], "float32"), "yt": ("sbuf", [128, C], "float32"),
+    "rows": ("sbuf", [128, C * (3 * ROWS + 1)], "bfloat16"), "sc": ("sbuf", [128, C * SLOTS], "float16"),
+    "tf": ("sbuf", [128, KT * 3 * TABS], "float32"), "tu": ("sbuf", [128, KT * 3 * SLOTS], "uint16"),
+}
+for r in range(4):
+    SCRATCH["xt%d" % r] = ("sbuf", [128, 4 * C], "bfloat16")
+    SCRATCH["q%d" % r] = ("sbuf", [128, C], "float8_e4m3fn_x4")
+    SCRATCH["qs%d" % r] = ("sbuf", [128, C], "uint8")
+for r in range(3):
+    for k in ("f", "zt", "h", "o"):
+        SCRATCH["%s%d" % (k, r)] = ("sbuf", [128, 4 * C], "bfloat16")
+    for k in ("lq", "zq"):
+        SCRATCH["%s%d" % (k, r)] = ("sbuf", [128, C], "float8_e4m3fn_x4")
+    for k in ("lp", "zp"):
+        SCRATCH["%s%d" % (k, r)] = ("sbuf", [128, C], "uint8")
+    SCRATCH["t1l%d" % r] = ("sbuf", [128, KT], "uint16")
+    SCRATCH["t2l%d" % r] = ("sbuf", [128, 2 * KT], "uint16")
+    for k in ("sf", "sr"):
+        SCRATCH["%s%d" % (k, r)] = ("sbuf", [128, C], "float32")
+for k in ("fd", "za", "zad", "zb", "zbd"):
+    SCRATCH[k] = ("sbuf", [128, 4 * C], "bfloat16")
+for r in range(8):
+    SCRATCH["pb%d" % r] = ("psum", [128, 512], "float32")
+SEMAPHORES = ["cv", "ca", "cp", "cg", "dx0", "dx1", "du", "dl", "dw", "dv", "sent", "out"] + ["%s%d" % (k, r) for k in ("aq", "at", "au") for r in range(3)]
+
+
+def rank_program(g, core, T, topo):
+    me = T.rank_of(core)
+    if me is None:
+        return
+    n_ranks = len(T.cores)
+    A, F = AluOpType, ActivationFunctionType
+    queues = {"v": g.vector, "a": g.scalar, "p": g.tensor, "g": g, "s": g.sync}
+    own = {"v": "cv", "a": "ca", "p": "cp", "g": "cg"}
+    total = {}
+    known = {q: {} for q in queues}
+    log = {}
+
+    def vw(name, a, n, step=1):
+        return (name, a, a + n * step, step)
+
+    def ap(v):
+        name, a, b, st = v
+        return T[name][:, a:b] if st == 1 else T[name][:, a:b - st + 1:st]
+
+    def wait(q, tok):
+        sem, n, clock = tok
+        if known[q].get(sem, 0) >= n:
+            return
+        queues[q].wait_ge(T.sem[sem], n)
+        known[q][sem] = n
+        for k in clock:
+            if clock[k] > known[q].get(k, 0):
+                known[q][k] = clock[k]
+
+    def order(q, kind, reads, writes):
+        deps = {}
+        for v, w in [(v, False) for v in reads] + [(v, True) for v in writes]:
+            name, a, b, st = v
+            bank = SCRATCH[name][0] == "psum"
+            for a2, b2, st2, w2, k2, tok in log.get(name, ()):
+                if k2 == kind and kind != "dma" and not (w2 and not w):
+                    continue
+                if not bank and (b2 <= a or b <= a2 or not (w or w2) or (st == st2 and st > 1 and (a - a2) % st)):
+                    continue
+                if tok[0] not in deps or deps[tok[0]][1] < tok[1]:
+                    deps[tok[0]] = tok
+        for sem in sorted(deps, key=lambda s: s == own.get(q)):
+            wait(q, deps[sem])
+
+    def note(kind, reads, writes, tok):
+        for v, w in [(v, False) for v in reads] + [(v, True) for v in writes]:
+            log.setdefault(v[0], []).append((v[1], v[2], v[3], w, kind, tok))
+
+    def do(q, make, reads, writes):
+        order(q, q, reads, writes)
+        sem = own[q]
+        total[sem] = total.get(sem, 0) + 1
+        make().then_inc(T.sem[sem], 1)
+        note(q, reads, writes, (sem, total[sem], dict(known[q])))
+
+    def dma(q, out, in_, sem, full, reads, writes):
+        order(q, "dma", reads, writes)
+        total[sem] = total.get(sem, 0) + 16
+        queues[q].dma_start(out, in_).then_inc(T.sem[sem], 16)
+        note("dma", reads, writes, (sem, full, dict(known[q])))
+
+    def ts(out, in0, s1, s2, op0, op1=None, off=None):
+        rd = [in0] + [s for s in (s1, s2) if isinstance(s, tuple)] + ([off] if off else [])
+        x1, x2 = [ap(s) if isinstance(s, tuple) else s for s in (s1, s2)]
+        src = ap(in0).indirect(ap(off)) if off else ap(in0)
+        if op1 is None:
+            do("v", lambda: g.vector.tensor_scalar(ap(out), src, x1, None, op0), rd, [out])
+        else:
+            do("v", lambda: g.vector.tensor_scalar(ap(out), src, x1, x2, op0, op1), rd, [out])
+
+    def tt(out, in0, in1, op, off=None):
+        src = ap(in0).indirect(ap(off)) if off else ap(in0)
+        do("v", lambda: g.vector.tensor_tensor(ap(out), src, ap(in1), op), [in0, in1] + ([off] if off else []), [out])
+
+    def tcopy(out, in_):
+        do("v", lambda: g.vector.tensor_copy(ap(out), ap(in_)), [in_], [out])
+
+    def act(out, in_, scale=1.0):
+        if scale == 1.0:
+            do("a", lambda: g.scalar.activation(ap(out), ap(in_), F.Copy), [in_], [out])
+        else:
+            do("a", lambda: g.scalar.activation(ap(out), ap(in_), F.Copy, scale=scale), [in_], [out])
+
+    def gather(q, out, win, off):
+        if q == "v":
+            do("v", lambda: g.vector.tensor_copy(ap(out), ap(win).indirect(ap(off))), [win, off], [out])
+        else:
+            do("a", lambda: g.scalar.activation(ap(out), ap(win).indirect(ap(off)), F.Copy), [win, off], [out])
+
+    def quant(q, s, tile, a, n, at=None):
+        t = vw(tile, 4 * a if at is None else at, 4 * n)
+        do("v", lambda: g.vector.quantize_mx(ap(vw(q, a, n)), ap(vw(s, a, n)), ap(t)), [t], [vw(q, a, n), vw(s, a, n)])
+
+    def mm(bank, lq, ls, la, rq, rs, ra, n):
+        o = vw("pb%d" % bank, 0, n)
+        rd = [vw(lq, la, 128), vw(ls, la, 128), vw(rq, ra, n), vw(rs, ra, n)]
+        do("p", lambda: g.tensor.matmul_mx(ap(o), ap(rd[0]), ap(rd[1]), ap(rd[2]), ap(rd[3]), True, True), rd, [o])
+        return o
+
+    def send(dst, out, in_, sem, codes=False):
+        order("g", "g", [in_], [])
+        rid, pid = topo.addr(dst)[:2]
+        o, i = (ap(out).bitcast(dt.uint8), ap(in_).bitcast(dt.uint8)) if codes else (ap(out), ap(in_))
+        g.remote_dma(o, i, T.sem[sem], T.sem.sent, pid, rid, topo.mask(core, dst))
+        total["sent"] = total.get("sent", 0) + len(topo.engines(core, dst))
+
+    nxt = {}
+
+    def place(buf, n):
+        a = nxt.get(buf, 0)
+        nxt[buf] = a + n
+        return a
+
+    def row():
+        return place("rows", C)
+
+    def rv(a, lo=0, n=C):
+        return vw("rows", a + lo, n)
+
+    def tab():
+        return vw("tf", place("tf", KT), KT)
+
+    def off(n=KT):
+        return vw("tu", place("tu", n), n)
+
+    def part(o, lo, n):
+        return (o[0], o[1] + lo, o[1] + lo + n, 1)
+
+    mask = "mask"
+
+    def scan(out, a, lo, n):
+        o = vw("sc", out + lo, n)
+        m, x = vw(mask, lo, n), rv(a, lo, n)
+        do("v", lambda: g.vector.tensor_tensor_scan(ap(o), ap(m), ap(x), 0.0, A.add, A.max), [m, x], [o])
+
+    def picked(s):
+        return vw("sc", s + 15, KT, 16)
+
+    col = {k: vw("cols", i, 1) for i, k in enumerate(("p15", "last", "k", "turn", "half_k", "one_2k"))}
+
+    def table(a, o):
+        s = place("sc", C)
+        scan(s, a, 0, C)
+        ts(o, picked(s), col["turn"], None, A.add)
+
+    dma("s", T.xt0[:, 0:2 * C], T.x[:, 0:2 * C], "dx0", 16, [], [vw("xt0", 0, 2 * C)])
+    dma("a", T.ut[:, :], T.u[:, :], "du", 16, [], [vw("ut", 0, 512)])
+    dma("s", T.xt0[:, 2 * C:4 * C], T.x[:, 2 * C:4 * C], "dx1", 16, [], [vw("xt0", 2 * C, 2 * C)])
+    dma("a", T.lai[:, :], T.la[:, :], "dl", 32, [], [vw("lai", 0, KT)])
+    dma("a", T.lbi[:, :], T.lb[:, :], "dl", 32, [], [vw("lbi", 0, KT)])
+    dma("s", T.wq[:, :].bitcast(dt.uint8), T.wc[:, :], "dw", 32, [], [vw("wq", 0, 512)])
+    dma("s", T.wp[:, :], T.ws[:, :], "dw", 32, [], [vw("wp", 0, 512)])
+    dma("s", T.vt[:, :], T.v[:, :], "dv", 16, [], [vw("vt", 0, 512)])
+
+    do("v", lambda: g.vector.memset(T.ones[:, :], 1.0), [], [vw("ones", 0, 528)])
+    do("g", lambda: g.iota(T.ip[:, :], [[16, 8]], 0, 0), [], [vw("ip", 0, 8)])
+    do("g", lambda: g.iota(T.ik[:, :], [[16, KT]], 0, 0), [], [vw("ik", 0, KT)])
+    do("g", lambda: g.iota(T.im[:, :], [[0, KT], [1, 16]], 128, -1), [], [vw("im", 0, C)])
+    ident = row()
+    do("g", lambda: g.iota(ap(rv(ident)), [[1, C]], -int(MID), 0, allow_small_or_imprecise_dtypes=True), [], [rv(ident)])
+    do("g", lambda: g.affine_select(T.et[:, :], T.ones[:, :], [[-1, 528]], A.is_equal, 0.0, 8, 4), [vw("ones", 0, 528)], [vw("et", 0, 528)])
+    do("g", lambda: g.iota(T.num[:, :], [[1, C]], 0, 0, allow_small_or_imprecise_dtypes=True), [], [vw("num", 0, C)])
+    tcopy(vw("plist", 0, 8), vw("ip", 0, 8))
+    im2 = vw("im2", 0, C)
+    ts(im2, vw("im", 0, C), 15, None, A.bitwise_and)
+    ts(vw("ma", 0, C), im2, 0, -BIG, A.is_equal, A.mult)
+    ts(vw("mb", 0, C), im2, 1, LIFT, A.is_equal, A.mult)
+    tt(vw(mask, 0, C), vw("ma", 0, C), vw("mb", 0, C), A.add)
+    z = tab()
+    zc = (z[0], z[1], z[1] + 1, 1)
+    ts(zc, vw("im2", 0, 1), 0, 16, A.not_equal, A.mult)
+    tt(col["p15"], zc, vw("im2", 0, 1), A.subtract)
+    ts(col["k"], vw("im2", 0, 1), 1, LIFT, A.not_equal, A.mult)
+    ts(col["turn"], col["k"], -1.0, MID, A.mult, A.add)
+    ts(col["half_k"], col["k"], 0.5, None, A.add)
+    ts(col["one_2k"], col["k"], 2.0, 1.0, A.mult, A.add)
+    num_t, low_t = tab(), tab()
+    ts(num_t, vw("ik", 0, KT), col["p15"], None, A.add)
+    ts(low_t, num_t, -MID, col["k"], A.add, A.add)
+    quant("qu", "qus", "ut", 0, 128)
+    do("v", lambda: g.vector.tensor_copy(T.qr[:, :].bitcast(dt.uint32), T.qu[:, :].bitcast(dt.uint32).indirect(T.plist[:, 0:8])), [vw("qu", 0, 128), vw("plist", 0, 8)], [vw("qr", 0, 128)])
+    do("a", lambda: g.scalar.activation(T.qrs[:, :], T.qus[:, :].indirect(T.plist[:, 0:8]), F.Copy), [vw("qus", 0, 128), vw("plist", 0, 8)], [vw("qrs", 0, 128)])
+    diff, base = tab(), tab()
+    lift = tab()
+    tt(diff, vw("lbi", 0, KT), vw("lai", 0, KT), A.subtract)
+    ts(lift, diff, col["k"], None, A.mult)
+    tt(base, vw("lai", 0, KT), lift, A.subtract)
+
+    S_BANK = (0, 7)
+    chg_s = None
+
+    def exchange(diff, base, s):
+        sg, d2, dd, e, b2 = tab(), tab(), tab(), tab(), tab()
+        ts(sg, picked(s), -2.0, col["one_2k"], A.mult, A.add)
+        tt(d2, diff, sg, A.mult)
+        tt(dd, diff, d2, A.subtract)
+        ts(e, dd, col["half_k"], None, A.mult)
+        tt(b2, base, e, A.add)
+        return d2, b2
+
+    for r, d in enumerate(STEPS):
+        last = r == len(STEPS) - 1
+        dst = T.cores[(me + d) % n_ranks]
+        q, qs, xt = "q%d" % r, "qs%d" % r, "xt%d" % r
+        lq, lp, t1l, t2l = "lq%d" % r, "lp%d" % r, "t1l%d" % r, "t2l%d" % r
+        src = T.cores[(me - d) % n_ranks]
+        ne = len(topo.engines(src, core))
+        total["aq%d" % r], total["at%d" % r], total["au%d" % r] = 2 * ne, ne, ne
+        note("dma", [], [vw(lq, 0, C), vw(lp, 0, C)], ("aq%d" % r, 2 * ne, {}))
+        note("dma", [], [vw(t1l, 0, KT)], ("at%d" % r, ne, {}))
+        note("dma", [], [vw(t2l, 0, 2 * KT)], ("au%d" % r, ne, {}))
+        f, zt, h, o = ["%s%d" % (k, r) for k in ("f", "zt", "h", "o")]
+        fd, za, zad, zb, zbd = "fd", "za", "zad", "zb", "zbd"
+        nxt["sc"] = 0
+
+        def plane(t, b, lo=0, n=C):
+            return vw(t, C * b + lo, n)
+
+        sv = []
+        for i in range(2):
+            quant(q, qs, xt, HALF * i, HALF)
+            sv.append(mm(S_BANK[i], "qr", "qrs", 0, q, qs, HALF * i, HALF))
+        send(dst, vw(lq, 0, C), vw(q, 0, C), "aq%d" % r, True)
+        send(dst, vw(lp, 0, C), vw(qs, 0, C), "aq%d" % r)
+        if chg_s is not None:
+            diff, base = exchange(diff, base, chg_s)
+        neg = row()
+        for i in range(2):
+            ts(rv(neg, HALF * i, HALF), sv[i], 0.0, None, A.is_lt)
+        s = place("sc", C)
+        scan(s, neg, 0, C)
+        w, p_t, to_self = tab(), tab(), tab()
+        tt(w, picked(s), diff, A.mult)
+        tt(p_t, w, base, A.add)
+        t_k = off()
+        tcopy(t_k, p_t)
+        at = row()
+        for qq, lo in (("v", 0), ("a", HALF)):
+            gather(qq, rv(at, lo, HALF), rv(ident), part(t_k, lo // 16, HALF // 16))
+        if r == 0:
+            for b in range(4):
+                quant("qe", "qes", "et", 128 * b, 128, 8 - b)
+        own_f = [mm(5 + b, "qe", "qes", 128 * b, q, qs, 0, C) for b in range(2)]
+
+        def copy_own(k):
+            b, lo = k // 2, HALF * (k % 2)
+            if len(own_f) <= b:
+                own_f.append(mm(3 + b, "qe", "qes", 128 * b, q, qs, 0, C))
+            v = own_f[b]
+            act(plane(o, b, lo, HALF), (v[0], lo, lo + HALF, 1))
+
+        tt(to_self, num_t, p_t, A.subtract)
+
+        low, twin = at, row()
+        tcopy(rv(twin), rv(at))
+        for k in range(7):
+            at2, low2, twin2, t2 = row(), row(), row(), off()
+            gather("a", rv(at2), rv(at), t_k)
+            copy_own(k)
+            tt(rv(low2), rv(low), rv(twin), A.min, t_k)
+            tcopy(rv(twin2), rv(low2))
+            table(at2, t2)
+            at, low, twin, t_k = at2, low2, twin2, t2
+        copy_own(7)
+        for b in range(4):
+            fb = mm(1 + b, "qe", "qes", 128 * b, lq, lp, 0, C)
+            act(plane(f, b), fb, 0.125)
+        low2, twin2, m = row(), row(), row()
+        tt(rv(low2), rv(low), rv(twin), A.min, t_k)
+        tcopy(rv(twin2, 0, 128), rv(low2, 0, 128))
+        tt(rv(m, 0, 128), rv(low2), rv(twin2, 0, 128), A.min, part(t_k, 0, 8))
+        s = place("sc", C)
+        o1, x1 = vw("sc", s + 128, C - 128), rv(low2, 128, C - 128)
+        mk = vw(mask, 128, C - 128)
+        do("v", lambda: g.vector.tensor_tensor_scan(ap(o1), ap(mk), ap(x1), 0.0, A.add, A.max), [mk, x1], [o1])
+        scan(s, m, 0, 128)
+        eq, mv, t_f, tears = tab(), tab(), tab(), off()
+        tt(eq, picked(s), low_t, A.is_equal)
+        tt(mv, eq, to_self, A.mult)
+        tt(t_f, mv, p_t, A.add)
+        tcopy(tears, t_f)
+        send(dst, vw(t1l, 0, KT), tears, "at%d" % r)
+
+        tr, tr2, tr4 = row(), row(), row()
+        both = off(2 * KT)
+        jump2, jump4 = part(both, 0, KT), part(both, KT, KT)
+        for out, win, o_ in ((tr, ident, tears), (tr2, tr, tears), (tr4, tr2, jump2)):
+            for qq, lo in (("v", 0), ("a", HALF)):
+                gather(qq, rv(out, lo, HALF), rv(win), part(o_, lo // 16, HALF // 16))
+            if out == tr2:
+                table(tr2, jump2)
+        table(tr4, jump4)
+        send(dst, vw(t2l, 0, 2 * KT), both, "au%d" % r)
+        tcopy(rv(twin2, 128, C - 128), rv(low2, 128, C - 128))
+        tt(rv(m, 128, C - 128), rv(low2), rv(twin2, 128, C - 128), A.min, part(t_k, 8, KT - 8))
+        if r == 0:
+            quant("qv", "qvs", "vt", 0, 128)
+        tcopy(plane(fd, 0), plane(f, 0))
+        for b in range(1, 4):
+            act(plane(fd, b), plane(f, b))
+
+        sf, sr = "sf%d" % r, "sr%d" % r
+        lead = [m, row(), row(), row()]
+        for b in range(4):
+            tt(plane(za, b), plane(f, b), plane(fd, b), A.add, vw(t1l, 0, KT))
+            act(plane(zad, b), plane(za, b))
+            if b < 2:
+                act(vw(sf, HALF * b, HALF), sv[b])
+            if b == 2:
+                gather("a", rv(lead[1]), rv(m), t_k)
+        for b in range(4):
+            tt(plane(zb, b), plane(za, b), plane(zad, b), A.add, vw(t2l, 0, KT))
+            if b in (1, 3):
+                gather("a", rv(lead[(b + 3) // 2]), rv(lead[(b + 1) // 2]), t_k)
+            act(plane(zbd, b), plane(zb, b))
+        for b in range(4):
+            tt(vw(zt, b, C, 4), plane(zb, b), plane(zbd, b), A.add, vw(t2l, KT, KT))
+            if b == 1:
+                t_r = off()
+                table(lead[3], t_r)
+                for i in range(2):
+                    gather("a", vw(sr, HALF * i, HALF), vw(sf, 0, C), part(t_r, HALF * i // 16, HALF // 16))
+        zq, zp = "zq%d" % r, "zp%d" % r
+        for i in range(2):
+            quant(zq, zp, zt, HALF * i, HALF)
+            hb = mm((1, 5)[i], "wq", "wp", 0, zq, zp, HALF * i, HALF)
+            act(plane(h, 0, HALF * i, HALF), hb, 0.03125)
+        for b in range(1, 4):
+            hb = mm(1 + b, "wq", "wp", 128 * b, zq, zp, 0, C)
+            act(plane(h, b), hb, 0.03125)
+        chg = row()
+        for i in range(2):
+            tt(rv(chg, HALF * i, HALF), sv[i], vw(sr, HALF * i, HALF), A.is_lt)
+        chg_s = place("sc", C)
+        scan(chg_s, chg, 0, C)
+
+        x2 = "xt%d" % (r + 1)
+        if not last:
+            for b in range(4):
+                tt(vw(x2, b, C, 4), plane(h, b), plane(o, b), A.add, tears)
+    q, qs = "q3", "qs3"
+    for i in range(2):
+        lo = HALF * i
+        for b in range(4):
+            tt(vw(x2, 4 * lo + b, HALF, 4), plane(h, b), plane(o, b, lo, HALF), A.add, part(tears, lo // 16, HALF // 16))
+        quant(q, qs, x2, lo, HALF)
+        yb = mm((0, 7)[i], "qv", "qvs", 0, q, qs, lo, HALF)
+        act(vw("yt", lo, HALF), yb)
+        qv = vw(q, lo, HALF)
+        dma("s", T.oc[:, 4 * lo:4 * lo + 4 * HALF], ap(qv).bitcast(dt.uint8), "out", 0, [qv], [])
+        for k in range(4):
+            dma("s", T.osc[4 * k:4 * k + 4, lo:lo + HALF], T[qs][32 * k:32 * k + 4, lo:lo + HALF], "out", 0, [vw(qs, lo, HALF)], [])
+        dma("a", T.y[:, lo:lo + HALF], ap(vw("yt", lo, HALF)), "out", 0, [vw("yt", lo, HALF)], [])
+        if i == 0:
+            diff, base = exchange(diff, base, chg_s)
+            lift, l0, l1 = tab(), tab(), tab()
+            ts(lift, diff, col["k"], None, A.mult)
+            tt(l0, lift, base, A.add)
+            tt(l1, l0, diff, A.add)
+            for j, l in enumerate((l0, l1)):
+                t = off()
+                tcopy(t, l)
+                gather("a", vw("lsr", C * j, C), vw("num", 0, C), t)
+            dma("s", T.ls[:, :], T.lsr[0:128:16, :], "out", 0, [vw("lsr", 0, 2 * C)], [])
+    for sem in sorted(total):
+        if known["g"].get(sem, 0) < total[sem]:
+            g.wait_ge(T.sem[sem], total[sem])

@@ -18,7 +18,8 @@ SCRATCH = {
     "ones": ("sbuf", [128, 528], "bfloat16"), "et": ("sbuf", [128, 528], "bfloat16"),
     "qe": ("sbuf", [128, 512], "float8_e4m3fn_x4"), "qes": ("sbuf", [128, 512], "uint8"),
     "lai": ("sbuf", [128, KT], "int32"), "lbi": ("sbuf", [128, KT], "int32"),
-    "im": ("sbuf", [128, C], "int32"), "im2": ("sbuf", [128, C], "int32"), "ma": ("sbuf", [128, C], "float32"), "mb": ("sbuf", [128, C], "bfloat16"),
+    "im": ("sbuf", [128, 16], "int32"), "im2": ("sbuf", [128, 16], "int32"), "ma": ("sbuf", [128, 16], "float32"), "mb": ("sbuf", [128, 16], "bfloat16"),
+    "et8": ("sbuf", [128, 528], "bfloat16"), "qe8": ("sbuf", [128, 256], "float8_e4m3fn_x4"), "qe8s": ("sbuf", [128, 256], "uint8"),
     "mask": ("sbuf", [128, C], "bfloat16"), "ik": ("sbuf", [128, KT], "int32"), "ip": ("sbuf", [128, 8], "int32"),
     "cols": ("sbuf", [128, 16], "float32"), "plist": ("sbuf", [128, 8], "uint16"),
     "num": ("sbuf", [128, C], "float32"), "lsr": ("sbuf", [128, 2 * C], "float32"), "yt": ("sbuf", [128, C], "float32"),
@@ -44,7 +45,7 @@ for k in ("fd", "za", "zad", "zb", "zbd"):
     SCRATCH[k] = ("sbuf", [128, 4 * C], "bfloat16")
 for r in range(8):
     SCRATCH["pb%d" % r] = ("psum", [128, 512], "float32")
-SEMAPHORES = ["cv", "ca", "cp", "cg", "dx0", "dx1", "du", "dl", "dw", "dv", "sent", "out"] + ["%s%d" % (k, r) for k in ("aq", "at", "au") for r in range(3)]
+SEMAPHORES = ["cv", "ca", "cp", "cg", "dx0", "dx1", "du", "dl", "dw", "dv", "sent", "out"] + ["%s%d" % (k, r) for k in ("aq", "at", "au", "av") for r in range(3)]
 
 
 def rank_program(g, core, T, topo):
@@ -130,6 +131,11 @@ def rank_program(g, core, T, topo):
         else:
             do("a", lambda: g.scalar.activation(ap(out), ap(in_), F.Copy, scale=scale), [in_], [out])
 
+    def twin_of(b, out, in_):
+        if b % 2 == 0:
+            return act(out, in_)
+        do("g", lambda: g.affine_select(ap(out), ap(in_), [[0, C]], A.is_gt, 0.0, 1, 0), [in_], [out])
+
     def gather(q, out, win, off):
         if q == "v":
             do("v", lambda: g.vector.tensor_copy(ap(out), ap(win).indirect(ap(off))), [win, off], [out])
@@ -197,24 +203,31 @@ def rank_program(g, core, T, topo):
     dma("s", T.xt0[:, 2 * C:4 * C], T.x[:, 2 * C:4 * C], "dx1", 16, [], [vw("xt0", 2 * C, 2 * C)])
     dma("a", T.lai[:, :], T.la[:, :], "dl", 32, [], [vw("lai", 0, KT)])
     dma("a", T.lbi[:, :], T.lb[:, :], "dl", 32, [], [vw("lbi", 0, KT)])
+    wait("s", ("dx0", 16, {}))
+    wait("s", ("dx1", 16, {}))
     dma("s", T.wq[:, :].bitcast(dt.uint8), T.wc[:, :], "dw", 32, [], [vw("wq", 0, 512)])
     dma("s", T.wp[:, :], T.ws[:, :], "dw", 32, [], [vw("wp", 0, 512)])
     dma("s", T.vt[:, :], T.v[:, :], "dv", 16, [], [vw("vt", 0, 512)])
 
     do("v", lambda: g.vector.memset(T.ones[:, :], 1.0), [], [vw("ones", 0, 528)])
+    do("g", lambda: g.iota(T.im[:, :], [[1, 16]], 128, -1), [], [vw("im", 0, 16)])
     do("g", lambda: g.iota(T.ip[:, :], [[16, 8]], 0, 0), [], [vw("ip", 0, 8)])
     do("g", lambda: g.iota(T.ik[:, :], [[16, KT]], 0, 0), [], [vw("ik", 0, KT)])
-    do("g", lambda: g.iota(T.im[:, :], [[0, KT], [1, 16]], 128, -1), [], [vw("im", 0, C)])
+    do("g", lambda: g.affine_select(T.et[:, :], T.ones[:, :], [[-1, 528]], A.is_equal, 0.0, 8, 4), [vw("ones", 0, 528)], [vw("et", 0, 528)])
     ident = row()
     do("g", lambda: g.iota(ap(rv(ident)), [[1, C]], -int(MID), 0, allow_small_or_imprecise_dtypes=True), [], [rv(ident)])
-    do("g", lambda: g.affine_select(T.et[:, :], T.ones[:, :], [[-1, 528]], A.is_equal, 0.0, 8, 4), [vw("ones", 0, 528)], [vw("et", 0, 528)])
     do("g", lambda: g.iota(T.num[:, :], [[1, C]], 0, 0, allow_small_or_imprecise_dtypes=True), [], [vw("num", 0, C)])
+    im2 = vw("im2", 0, 16)
+    ts(im2, vw("im", 0, 16), 15, None, A.bitwise_and)
     tcopy(vw("plist", 0, 8), vw("ip", 0, 8))
-    im2 = vw("im2", 0, C)
-    ts(im2, vw("im", 0, C), 15, None, A.bitwise_and)
-    ts(vw("ma", 0, C), im2, 0, -BIG, A.is_equal, A.mult)
-    ts(vw("mb", 0, C), im2, 1, LIFT, A.is_equal, A.mult)
-    tt(vw(mask, 0, C), vw("ma", 0, C), vw("mb", 0, C), A.add)
+    ts(vw("ma", 0, 16), im2, 0, -BIG, A.is_equal, A.mult)
+    ts(vw("mb", 0, 16), im2, 1, LIFT, A.is_equal, A.mult)
+    tt(vw(mask, 0, 16), vw("ma", 0, 16), vw("mb", 0, 16), A.add)
+    n = 16
+    while n < C:
+        m = min(n, C - n)
+        tcopy(vw(mask, n, m), vw(mask, 0, m))
+        n += m
     z = tab()
     zc = (z[0], z[1], z[1] + 1, 1)
     ts(zc, vw("im2", 0, 1), 0, 16, A.not_equal, A.mult)
@@ -229,6 +242,9 @@ def rank_program(g, core, T, topo):
     quant("qu", "qus", "ut", 0, 128)
     do("v", lambda: g.vector.tensor_copy(T.qr[:, :].bitcast(dt.uint32), T.qu[:, :].bitcast(dt.uint32).indirect(T.plist[:, 0:8])), [vw("qu", 0, 128), vw("plist", 0, 8)], [vw("qr", 0, 128)])
     do("a", lambda: g.scalar.activation(T.qrs[:, :], T.qus[:, :].indirect(T.plist[:, 0:8]), F.Copy), [vw("qus", 0, 128), vw("plist", 0, 8)], [vw("qrs", 0, 128)])
+    act(vw("et8", 0, 528), vw("et", 0, 528), 0.125)
+    for b in range(4):
+        quant("qe", "qes", "et", 128 * b, 128, 8 - b)
     diff, base = tab(), tab()
     lift = tab()
     tt(diff, vw("lbi", 0, KT), vw("lai", 0, KT), A.subtract)
@@ -240,12 +256,8 @@ def rank_program(g, core, T, topo):
 
     def exchange(diff, base, s):
         sg, d2, dd, e, b2 = tab(), tab(), tab(), tab(), tab()
-        ts(sg, picked(s), -2.0, col["one_2k"], A.mult, A.add)
-        tt(d2, diff, sg, A.mult)
-        tt(dd, diff, d2, A.subtract)
-        ts(e, dd, col["half_k"], None, A.mult)
-        tt(b2, base, e, A.add)
-        return d2, b2
+        return [lambda: ts(sg, picked(s), -2.0, col["one_2k"], A.mult, A.add), lambda: tt(d2, diff, sg, A.mult), lambda: tt(dd, diff, d2, A.subtract),
+                lambda: ts(e, dd, col["half_k"], None, A.mult), lambda: tt(b2, base, e, A.add), d2, b2]
 
     for r, d in enumerate(STEPS):
         last = r == len(STEPS) - 1
@@ -257,9 +269,11 @@ def rank_program(g, core, T, topo):
         total["aq%d" % r], total["at%d" % r], total["au%d" % r] = 2 * ne, ne, ne
         note("dma", [], [vw(lq, 0, C), vw(lp, 0, C)], ("aq%d" % r, 2 * ne, {}))
         note("dma", [], [vw(t1l, 0, KT)], ("at%d" % r, ne, {}))
-        note("dma", [], [vw(t2l, 0, 2 * KT)], ("au%d" % r, ne, {}))
+        total["av%d" % r] = ne
+        note("dma", [], [vw(t2l, 0, KT)], ("au%d" % r, ne, {}))
+        note("dma", [], [vw(t2l, KT, KT)], ("av%d" % r, ne, {}))
         f, zt, h, o = ["%s%d" % (k, r) for k in ("f", "zt", "h", "o")]
-        fd, za, zad, zb, zbd = "fd", "za", "zad", "zb", "zbd"
+        fd, za, zad, zb, zbd, hg = "fd", "za", "zad", "zb", "zbd", "zbd"
         nxt["sc"] = 0
 
         def plane(t, b, lo=0, n=C):
@@ -271,11 +285,17 @@ def rank_program(g, core, T, topo):
             sv.append(mm(S_BANK[i], "qr", "qrs", 0, q, qs, HALF * i, HALF))
         send(dst, vw(lq, 0, C), vw(q, 0, C), "aq%d" % r, True)
         send(dst, vw(lp, 0, C), vw(qs, 0, C), "aq%d" % r)
-        if chg_s is not None:
-            diff, base = exchange(diff, base, chg_s)
         neg = row()
+        if chg_s is not None:
+            xs = exchange(diff, base, chg_s)
+            for n in range(3):
+                xs[n]()
         for i in range(2):
             ts(rv(neg, HALF * i, HALF), sv[i], 0.0, None, A.is_lt)
+            if chg_s is not None:
+                xs[3 + i]()
+        if chg_s is not None:
+            diff, base = xs[5], xs[6]
         s = place("sc", C)
         scan(s, neg, 0, C)
         w, p_t, to_self = tab(), tab(), tab()
@@ -286,17 +306,18 @@ def rank_program(g, core, T, topo):
         at = row()
         for qq, lo in (("v", 0), ("a", HALF)):
             gather(qq, rv(at, lo, HALF), rv(ident), part(t_k, lo // 16, HALF // 16))
-        if r == 0:
-            for b in range(4):
-                quant("qe", "qes", "et", 128 * b, 128, 8 - b)
+        sf, sr = "sf%d" % r, "sr%d" % r
         own_f = [mm(5 + b, "qe", "qes", 128 * b, q, qs, 0, C) for b in range(2)]
 
         def copy_own(k):
             b, lo = k // 2, HALF * (k % 2)
-            if len(own_f) <= b:
-                own_f.append(mm(3 + b, "qe", "qes", 128 * b, q, qs, 0, C))
-            v = own_f[b]
-            act(plane(o, b, lo, HALF), (v[0], lo, lo + HALF, 1))
+            if k == 6:
+                act(vw(sf, 0, HALF), sv[0])
+            else:
+                act(plane(o, b, lo, HALF), part(own_f[b], lo, HALF))
+            if k in (1, 3):
+                b2 = 2 + k // 2
+                own_f.append(mm(3 + b2, "qe", "qes", 128 * b2, q, qs, 0, C))
 
         tt(to_self, num_t, p_t, A.subtract)
 
@@ -307,21 +328,29 @@ def rank_program(g, core, T, topo):
             gather("a", rv(at2), rv(at), t_k)
             copy_own(k)
             tt(rv(low2), rv(low), rv(twin), A.min, t_k)
-            tcopy(rv(twin2), rv(low2))
             table(at2, t2)
+            tcopy(rv(twin2), rv(low2))
             at, low, twin, t_k = at2, low2, twin2, t2
-        copy_own(7)
+        act(vw(sf, HALF, HALF), sv[1])
+        if r == 0:
+            for b in range(2):
+                quant("qe8", "qe8s", "et8", 128 * b, 128, 6 - b)
+        fp = []
         for b in range(4):
-            fb = mm(1 + b, "qe", "qes", 128 * b, lq, lp, 0, C)
-            act(plane(f, b), fb, 0.125)
+            if b < 2:
+                fp.append(mm(1 + b, "qe", "qes", 128 * b, lq, lp, 0, C))
+                act(plane(f, b), fp[b], 0.125)
+            else:
+                fp.append(mm(1 + b, "qe8", "qe8s", 128 * (b - 2), lq, lp, 0, C))
+                act(plane(f, b), fp[b])
         low2, twin2, m = row(), row(), row()
         tt(rv(low2), rv(low), rv(twin), A.min, t_k)
         tcopy(rv(twin2, 0, 128), rv(low2, 0, 128))
-        tt(rv(m, 0, 128), rv(low2), rv(twin2, 0, 128), A.min, part(t_k, 0, 8))
         s = place("sc", C)
         o1, x1 = vw("sc", s + 128, C - 128), rv(low2, 128, C - 128)
         mk = vw(mask, 128, C - 128)
         do("v", lambda: g.vector.tensor_tensor_scan(ap(o1), ap(mk), ap(x1), 0.0, A.add, A.max), [mk, x1], [o1])
+        tt(rv(m, 0, 128), rv(low2), rv(twin2, 0, 128), A.min, part(t_k, 0, 8))
         scan(s, m, 0, 128)
         eq, mv, t_f, tears = tab(), tab(), tab(), off()
         tt(eq, picked(s), low_t, A.is_equal)
@@ -338,33 +367,36 @@ def rank_program(g, core, T, topo):
                 gather(qq, rv(out, lo, HALF), rv(win), part(o_, lo // 16, HALF // 16))
             if out == tr2:
                 table(tr2, jump2)
+                send(dst, vw(t2l, 0, KT), jump2, "au%d" % r)
         table(tr4, jump4)
-        send(dst, vw(t2l, 0, 2 * KT), both, "au%d" % r)
+        send(dst, vw(t2l, KT, KT), jump4, "av%d" % r)
         tcopy(rv(twin2, 128, C - 128), rv(low2, 128, C - 128))
         tt(rv(m, 128, C - 128), rv(low2), rv(twin2, 128, C - 128), A.min, part(t_k, 8, KT - 8))
         if r == 0:
             quant("qv", "qvs", "vt", 0, 128)
-        tcopy(plane(fd, 0), plane(f, 0))
-        for b in range(1, 4):
+        for b in range(2):
             act(plane(fd, b), plane(f, b))
+        act(plane(o, 3, 0, HALF), part(own_f[3], 0, HALF))
 
-        sf, sr = "sf%d" % r, "sr%d" % r
         lead = [m, row(), row(), row()]
+        for b in range(2, 4):
+            gather("a", plane(fd, b), plane(f, b), vw(t1l, 0, KT))
         for b in range(4):
-            tt(plane(za, b), plane(f, b), plane(fd, b), A.add, vw(t1l, 0, KT))
-            act(plane(zad, b), plane(za, b))
             if b < 2:
-                act(vw(sf, HALF * b, HALF), sv[b])
-            if b == 2:
-                gather("a", rv(lead[1]), rv(m), t_k)
+                tt(plane(za, b), plane(f, b), plane(fd, b), A.add, vw(t1l, 0, KT))
+            else:
+                tt(plane(za, b), fp[b], plane(fd, b), A.add)
+            twin_of(b, plane(zad, b), plane(za, b))
+        gather("a", rv(lead[1]), rv(m), t_k)
         for b in range(4):
             tt(plane(zb, b), plane(za, b), plane(zad, b), A.add, vw(t2l, 0, KT))
-            if b in (1, 3):
-                gather("a", rv(lead[(b + 3) // 2]), rv(lead[(b + 1) // 2]), t_k)
-            act(plane(zbd, b), plane(zb, b))
+            if b == 1:
+                gather("a", rv(lead[2]), rv(lead[1]), t_k)
+            twin_of(b, plane(zbd, b), plane(zb, b))
+        gather("a", rv(lead[3]), rv(lead[2]), t_k)
         for b in range(4):
             tt(vw(zt, b, C, 4), plane(zb, b), plane(zbd, b), A.add, vw(t2l, KT, KT))
-            if b == 1:
+            if b == 2:
                 t_r = off()
                 table(lead[3], t_r)
                 for i in range(2):
@@ -385,23 +417,33 @@ def rank_program(g, core, T, topo):
 
         x2 = "xt%d" % (r + 1)
         if not last:
-            for b in range(4):
+            gather("a", plane(hg, 3, HALF, HALF), plane(h, 3), part(tears, KT // 2, KT // 2))
+            for b in range(3):
                 tt(vw(x2, b, C, 4), plane(h, b), plane(o, b), A.add, tears)
+            tt(vw(x2, 3, HALF, 4), plane(h, 3), plane(o, 3, 0, HALF), A.add, part(tears, 0, KT // 2))
+            tt(vw(x2, 4 * HALF + 3, HALF, 4), part(own_f[3], HALF, HALF), plane(hg, 3, HALF, HALF), A.add)
     q, qs = "q3", "qs3"
     for i in range(2):
         lo = HALF * i
-        for b in range(4):
+        if i == 0:
+            gather("a", plane(hg, 3, HALF, HALF), plane(h, 3), part(tears, KT // 2, KT // 2))
+        for b in range(4 - i):
             tt(vw(x2, 4 * lo + b, HALF, 4), plane(h, b), plane(o, b, lo, HALF), A.add, part(tears, lo // 16, HALF // 16))
+        if i == 1:
+            tt(vw(x2, 4 * lo + 3, HALF, 4), part(own_f[3], lo, HALF), plane(hg, 3, lo, HALF), A.add)
         quant(q, qs, x2, lo, HALF)
         yb = mm((0, 7)[i], "qv", "qvs", 0, q, qs, lo, HALF)
-        act(vw("yt", lo, HALF), yb)
         qv = vw(q, lo, HALF)
         dma("s", T.oc[:, 4 * lo:4 * lo + 4 * HALF], ap(qv).bitcast(dt.uint8), "out", 0, [qv], [])
         for k in range(4):
-            dma("s", T.osc[4 * k:4 * k + 4, lo:lo + HALF], T[qs][32 * k:32 * k + 4, lo:lo + HALF], "out", 0, [vw(qs, lo, HALF)], [])
+            dma("sa"[k // 2] if i else "s", T.osc[4 * k:4 * k + 4, lo:lo + HALF], T[qs][32 * k:32 * k + 4, lo:lo + HALF], "out", 0, [vw(qs, lo, HALF)], [])
+        act(vw("yt", lo, HALF), yb)
         dma("a", T.y[:, lo:lo + HALF], ap(vw("yt", lo, HALF)), "out", 0, [vw("yt", lo, HALF)], [])
         if i == 0:
-            diff, base = exchange(diff, base, chg_s)
+            xs = exchange(diff, base, chg_s)
+            for n in range(5):
+                xs[n]()
+            diff, base = xs[5], xs[6]
             lift, l0, l1 = tab(), tab(), tab()
             ts(lift, diff, col["k"], None, A.mult)
             tt(l0, lift, base, A.add)

@@ -5,6 +5,7 @@ C = 384
 HALF = C // 2
 STEPS = [1, 2, 3]
 KT = C // 16
+TWIN = 128
 ROWS = 34
 SLOTS = 14
 TABS = 20
@@ -239,17 +240,14 @@ def rank_program(g, core, T, topo):
     num_t, low_t = tab(), tab()
     ts(num_t, vw("ik", 0, KT), col["p15"], None, A.add)
     ts(low_t, num_t, -MID, col["k"], A.add, A.add)
+    for b in range(4):
+        quant("qe", "qes", "et", 128 * b, 128, 8 - b)
     quant("qu", "qus", "ut", 0, 128)
     do("v", lambda: g.vector.tensor_copy(T.qr[:, :].bitcast(dt.uint32), T.qu[:, :].bitcast(dt.uint32).indirect(T.plist[:, 0:8])), [vw("qu", 0, 128), vw("plist", 0, 8)], [vw("qr", 0, 128)])
     do("a", lambda: g.scalar.activation(T.qrs[:, :], T.qus[:, :].indirect(T.plist[:, 0:8]), F.Copy), [vw("qus", 0, 128), vw("plist", 0, 8)], [vw("qrs", 0, 128)])
     act(vw("et8", 0, 528), vw("et", 0, 528), 0.125)
-    for b in range(4):
-        quant("qe", "qes", "et", 128 * b, 128, 8 - b)
     diff, base = tab(), tab()
     lift = tab()
-    tt(diff, vw("lbi", 0, KT), vw("lai", 0, KT), A.subtract)
-    ts(lift, diff, col["k"], None, A.mult)
-    tt(base, vw("lai", 0, KT), lift, A.subtract)
 
     S_BANK = (0, 7)
     chg_s = None
@@ -286,6 +284,11 @@ def rank_program(g, core, T, topo):
         send(dst, vw(lq, 0, C), vw(q, 0, C), "aq%d" % r, True)
         send(dst, vw(lp, 0, C), vw(qs, 0, C), "aq%d" % r)
         neg = row()
+        if r == 0:
+            tt(diff, vw("lbi", 0, KT), vw("lai", 0, KT), A.subtract)
+            for b in range(2):
+                quant("qe8", "qe8s", "et8", 128 * b, 128, 6 - b)
+            ts(lift, diff, col["k"], None, A.mult)
         if chg_s is not None:
             xs = exchange(diff, base, chg_s)
             for n in range(3):
@@ -294,6 +297,8 @@ def rank_program(g, core, T, topo):
             ts(rv(neg, HALF * i, HALF), sv[i], 0.0, None, A.is_lt)
             if chg_s is not None:
                 xs[3 + i]()
+            elif i == 0:
+                tt(base, vw("lai", 0, KT), lift, A.subtract)
         if chg_s is not None:
             diff, base = xs[5], xs[6]
         s = place("sc", C)
@@ -328,13 +333,13 @@ def rank_program(g, core, T, topo):
             gather("a", rv(at2), rv(at), t_k)
             copy_own(k)
             tt(rv(low2), rv(low), rv(twin), A.min, t_k)
-            table(at2, t2)
-            tcopy(rv(twin2), rv(low2))
+            ss = place("sc", C)
+            scan(ss, at2, 0, C)
+            tcopy(rv(twin2, 0, TWIN), rv(low2, 0, TWIN))
+            ts(t2, picked(ss), col["turn"], None, A.add)
+            tcopy(rv(twin2, TWIN, C - TWIN), rv(low2, TWIN, C - TWIN))
             at, low, twin, t_k = at2, low2, twin2, t2
         act(vw(sf, HALF, HALF), sv[1])
-        if r == 0:
-            for b in range(2):
-                quant("qe8", "qe8s", "et8", 128 * b, 128, 6 - b)
         fp = []
         for b in range(4):
             if b < 2:
@@ -362,21 +367,20 @@ def rank_program(g, core, T, topo):
         tr, tr2, tr4 = row(), row(), row()
         both = off(2 * KT)
         jump2, jump4 = part(both, 0, KT), part(both, KT, KT)
-        for out, win, o_ in ((tr, ident, tears), (tr2, tr, tears), (tr4, tr2, jump2)):
+        for out, win in ((tr, ident), (tr2, tr)):
             for qq, lo in (("v", 0), ("a", HALF)):
-                gather(qq, rv(out, lo, HALF), rv(win), part(o_, lo // 16, HALF // 16))
-            if out == tr2:
-                table(tr2, jump2)
-                send(dst, vw(t2l, 0, KT), jump2, "au%d" % r)
-        table(tr4, jump4)
-        send(dst, vw(t2l, KT, KT), jump4, "av%d" % r)
+                gather(qq, rv(out, lo, HALF), rv(win), part(tears, lo // 16, HALF // 16))
+        act(plane(fd, 0), plane(f, 0))
+        table(tr2, jump2)
+        send(dst, vw(t2l, 0, KT), jump2, "au%d" % r)
+        gather("a", rv(tr4), rv(tr2), jump2)
         tcopy(rv(twin2, 128, C - 128), rv(low2, 128, C - 128))
         tt(rv(m, 128, C - 128), rv(low2), rv(twin2, 128, C - 128), A.min, part(t_k, 8, KT - 8))
+        table(tr4, jump4)
+        send(dst, vw(t2l, KT, KT), jump4, "av%d" % r)
         if r == 0:
             quant("qv", "qvs", "vt", 0, 128)
-        for b in range(2):
-            act(plane(fd, b), plane(f, b))
-        act(plane(o, 3, 0, HALF), part(own_f[3], 0, HALF))
+        act(plane(fd, 1), plane(f, 1))
 
         lead = [m, row(), row(), row()]
         for b in range(2, 4):
@@ -388,6 +392,7 @@ def rank_program(g, core, T, topo):
                 tt(plane(za, b), fp[b], plane(fd, b), A.add)
             twin_of(b, plane(zad, b), plane(za, b))
         gather("a", rv(lead[1]), rv(m), t_k)
+        act(plane(o, 3, 0, HALF), part(own_f[3], 0, HALF))
         for b in range(4):
             tt(plane(zb, b), plane(za, b), plane(zad, b), A.add, vw(t2l, 0, KT))
             if b == 1:
@@ -427,32 +432,33 @@ def rank_program(g, core, T, topo):
         lo = HALF * i
         if i == 0:
             gather("a", plane(hg, 3, HALF, HALF), plane(h, 3), part(tears, KT // 2, KT // 2))
+            xs = exchange(diff, base, chg_s)
+            d2, b2 = xs[5], xs[6]
+            lift, l0, l1, t0, t1 = tab(), tab(), tab(), off(), off()
+            steps = xs[:5] + [lambda: ts(lift, d2, col["k"], None, A.mult), lambda: tt(l0, lift, b2, A.add), lambda: tcopy(t0, l0),
+                              lambda: tt(l1, l0, d2, A.add), lambda: tcopy(t1, l1)]
         for b in range(4 - i):
             tt(vw(x2, 4 * lo + b, HALF, 4), plane(h, b), plane(o, b, lo, HALF), A.add, part(tears, lo // 16, HALF // 16))
+            steps.pop(0)()
         if i == 1:
+            for n, t in enumerate((t0, t1)):
+                gather("a", vw("lsr", C * n, C), vw("num", 0, C), t)
             tt(vw(x2, 4 * lo + 3, HALF, 4), part(own_f[3], lo, HALF), plane(hg, 3, lo, HALF), A.add)
         quant(q, qs, x2, lo, HALF)
         yb = mm((0, 7)[i], "qv", "qvs", 0, q, qs, lo, HALF)
         qv = vw(q, lo, HALF)
         dma("s", T.oc[:, 4 * lo:4 * lo + 4 * HALF], ap(qv).bitcast(dt.uint8), "out", 0, [qv], [])
         for k in range(4):
-            dma("sa"[k // 2] if i else "s", T.osc[4 * k:4 * k + 4, lo:lo + HALF], T[qs][32 * k:32 * k + 4, lo:lo + HALF], "out", 0, [vw(qs, lo, HALF)], [])
-        act(vw("yt", lo, HALF), yb)
-        dma("a", T.y[:, lo:lo + HALF], ap(vw("yt", lo, HALF)), "out", 0, [vw("yt", lo, HALF)], [])
+            dma("s", T.osc[4 * k:4 * k + 4, lo:lo + HALF], T[qs][32 * k:32 * k + 4, lo:lo + HALF], "out", 0, [vw(qs, lo, HALF)], [])
+        yv = vw("yt", lo, HALF)
         if i == 0:
-            xs = exchange(diff, base, chg_s)
-            for n in range(5):
-                xs[n]()
-            diff, base = xs[5], xs[6]
-            lift, l0, l1 = tab(), tab(), tab()
-            ts(lift, diff, col["k"], None, A.mult)
-            tt(l0, lift, base, A.add)
-            tt(l1, l0, diff, A.add)
-            for j, l in enumerate((l0, l1)):
-                t = off()
-                tcopy(t, l)
-                gather("a", vw("lsr", C * j, C), vw("num", 0, C), t)
-            dma("s", T.ls[:, :], T.lsr[0:128:16, :], "out", 0, [vw("lsr", 0, 2 * C)], [])
+            act(yv, yb)
+            for n in range(3):
+                steps.pop(0)()
+        else:
+            ts(yv, yb, 1.0, None, A.mult)
+        dma("as"[i], T.y[:, lo:lo + HALF], ap(yv), "out", 0, [yv], [])
+    dma("a", T.ls[:, :], T.lsr[0:128:16, :], "out", 0, [vw("lsr", 0, 2 * C)], [])
     for sem in sorted(total):
         if known["g"].get(sem, 0) < total[sem]:
             g.wait_ge(T.sem[sem], total[sem])

from concourse.bass import DstId, RemoteDMATransfer
from concourse.mybir import dt, AluOpType, ActivationFunctionType

C = 384
HALF = C // 2
STEPS = [1, 2, 3]
KT = C // 16
TWIN = 128
ROWS = 34
SLOTS = 14
TABS = 20
BIG, LIFT, MID = 2048.0, 512.0, 192.0

SCRATCH = {
    "ut": ("sbuf", [128, 512], "bfloat16"), "qu": ("sbuf", [128, 128], "float8_e4m3fn_x4"), "qus": ("sbuf", [128, 128], "uint8"),
    "qr": ("sbuf", [128, 128], "float8_e4m3fn_x4"), "qrs": ("sbuf", [128, 128], "uint8"),
    "vt": ("sbuf", [128, 512], "bfloat16"), "qv": ("sbuf", [128, 128], "float8_e4m3fn_x4"), "qvs": ("sbuf", [128, 128], "uint8"),
    "wq": ("sbuf", [128, 512], "float8_e4m3fn_x4"), "wp": ("sbuf", [128, 512], "uint8"),
    "ones": ("sbuf", [128, 528], "bfloat16"), "et": ("sbuf", [128, 528], "bfloat16"),
    "qe": ("sbuf", [128, 512], "float8_e4m3fn_x4"), "qes": ("sbuf", [128, 512], "uint8"),
    "lai": ("sbuf", [128, KT], "int32"), "lbi": ("sbuf", [128, KT], "int32"),
    "im": ("sbuf", [128, 16], "int32"), "im2": ("sbuf", [128, 16], "int32"), "ma": ("sbuf", [128, 16], "float32"), "mb": ("sbuf", [128, 16], "bfloat16"),
    "et8": ("sbuf", [128, 528], "bfloat16"), "qe8": ("sbuf", [128, 256], "float8_e4m3fn_x4"), "qe8s": ("sbuf", [128, 256], "uint8"),
    "mask": ("sbuf", [128, C], "bfloat16"), "ik": ("sbuf", [128, KT], "int32"), "ip": ("sbuf", [128, 8], "int32"),
    "cols": ("sbuf", [128, 16], "float32"), "plist": ("sbuf", [128, 8], "uint16"),
    "num": ("sbuf", [128, C], "float32"), "lsr": ("sbuf", [128, 2 * C], "float32"), "yt": ("sbuf", [128, C], "float32"),
    "rows": ("sbuf", [128, C * (3 * ROWS + 1)], "bfloat16"), "sc": ("sbuf", [128, C * SLOTS], "float16"),
    "tf": ("sbuf", [128, KT * 3 * TABS], "float32"), "tu": ("sbuf", [128, KT * 3 * SLOTS], "uint16"),
}
for r in range(4):
    SCRATCH["xt%d" % r] = ("sbuf", [128, 4 * C], "bfloat16")
    SCRATCH["q%d" % r] = ("sbuf", [128, C], "float8_e4m3fn_x4")
    SCRATCH["qs%d" % r] = ("sbuf", [128, C], "uint8")
for r in range(3):
    for k in ("f", "zt", "h", "o"):
        SCRATCH["%s%d" % (k, r)] = ("sbuf", [128, 4 * C], "bfloat16")
    for k in ("lq", "zq"):
        SCRATCH["%s%d" % (k, r)] = ("sbuf", [128, C], "float8_e4m3fn_x4")
    for k in ("lp", "zp"):
        SCRATCH["%s%d" % (k, r)] = ("sbuf", [128, C], "uint8")
    SCRATCH["t1l%d" % r] = ("sbuf", [128, KT], "uint16")
    SCRATCH["t2l%d" % r] = ("sbuf", [128, 2 * KT], "uint16")
    for k in ("sf", "sr"):
        SCRATCH["%s%d" % (k, r)] = ("sbuf", [128, C], "float32")
for k in ("fd", "za", "zad", "zb", "zbd"):
    SCRATCH[k] = ("sbuf", [128, 4 * C], "bfloat16")
for r in range(8):
    SCRATCH["pb%d" % r] = ("psum", [128, 512], "float32")
SEMAPHORES = ["cv", "ca", "cp", "cg", "dx0", "dx1", "du", "dl", "dw", "dv", "sent", "out"] + ["%s%d" % (k, r) for k in ("aq", "at", "au", "av") for r in range(3)]


def rank_program(g, core, T, topo):
    me = T.rank_of(core)
    if me is None:
        return
    n_ranks = len(T.cores)
    A, F = AluOpType, ActivationFunctionType
    queues = {"v": g.vector, "a": g.scalar, "p": g.tensor, "g": g, "s": g.sync}
    own = {"v": "cv", "a": "ca", "p": "cp", "g": "cg"}
    total = {}
    known = {q: {} for q in queues}
    log = {}

    def vw(name, a, n, step=1):
        return (name, a, a + n * step, step)

    def ap(v):
        name, a, b, st = v
        return T[name][:, a:b] if st == 1 else T[name][:, a:b - st + 1:st]

    def wait(q, tok):
        sem, n, clock = tok
        if known[q].get(sem, 0) >= n:
            return
        queues[q].wait_ge(T.sem[sem], n)
        known[q][sem] = n
        for k in clock:
            if clock[k] > known[q].get(k, 0):
                known[q][k] = clock[k]

    def order(q, kind, reads, writes):
        deps = {}
        for v, w in [(v, False) for v in reads] + [(v, True) for v in writes]:
            name, a, b, st = v
            bank = SCRATCH[name][0] == "psum"
            for a2, b2, st2, w2, k2, tok in log.get(name, ()):
                if k2 == kind and kind != "dma" and not (w2 and not w):
                    continue
                if not bank and (b2 <= a or b <= a2 or not (w or w2) or (st == st2 and st > 1 and (a - a2) % st)):
                    continue
                if tok[0] not in deps or deps[tok[0]][1] < tok[1]:
                    deps[tok[0]] = tok
        for sem in sorted(deps, key=lambda s: s == own.get(q)):
            wait(q, deps[sem])

    def note(kind, reads, writes, tok):
        for v, w in [(v, False) for v in reads] + [(v, True) for v in writes]:
            log.setdefault(v[0], []).append((v[1], v[2], v[3], w, kind, tok))

    def do(q, make, reads, writes):
        order(q, q, reads, writes)
        sem = own[q]
        total[sem] = total.get(sem, 0) + 1
        make().then_inc(T.sem[sem], 1)
        note(q, reads, writes, (sem, total[sem], dict(known[q])))

    def dma(q, out, in_, sem, full, reads, writes):
        order(q, "dma", reads, writes)
        total[sem] = total.get(sem, 0) + 16
        queues[q].dma_start(out, in_).then_inc(T.sem[sem], 16)
        note("dma", reads, writes, (sem, full, dict(known[q])))

    def ts(out, in0, s1, s2, op0, op1=None, off=None):
        rd = [in0] + [s for s in (s1, s2) if isinstance(s, tuple)] + ([off] if off else [])
        x1, x2 = [ap(s) if isinstance(s, tuple) else s for s in (s1, s2)]
        src = ap(in0).indirect(ap(off)) if off else ap(in0)
        if op1 is None:
            do("v", lambda: g.vector.tensor_scalar(ap(out), src, x1, None, op0), rd, [out])
        else:
            do("v", lambda: g.vector.tensor_scalar(ap(out), src, x1, x2, op0, op1), rd, [out])

    def tt(out, in0, in1, op, off=None):
        src = ap(in0).indirect(ap(off)) if off else ap(in0)
        do("v", lambda: g.vector.tensor_tensor(ap(out), src, ap(in1), op), [in0, in1] + ([off] if off else []), [out])

    def tcopy(out, in_):
        do("v", lambda: g.vector.tensor_copy(ap(out), ap(in_)), [in_], [out])

    def act(out, in_, scale=1.0):
        if scale == 1.0:
            do("a", lambda: g.scalar.activation(ap(out), ap(in_), F.Copy), [in_], [out])
        else:
            do("a", lambda: g.scalar.activation(ap(out), ap(in_), F.Copy, scale=scale), [in_], [out])

    def twin_of(b, out, in_):
        if b % 2 == 0:
            return act(out, in_)
        do("g", lambda: g.affine_select(ap(out), ap(in_), [[0, C]], A.is_gt, 0.0, 1, 0), [in_], [out])

    def gather(q, out, win, off):
        if q == "v":
            do("v", lambda: g.vector.tensor_copy(ap(out), ap(win).indirect(ap(off))), [win, off], [out])
        else:
            do("a", lambda: g.scalar.activation(ap(out), ap(win).indirect(ap(off)), F.Copy), [win, off], [out])

    def quant(q, s, tile, a, n, at=None):
        t = vw(tile, 4 * a if at is None else at, 4 * n)
        do("v", lambda: g.vector.quantize_mx(ap(vw(q, a, n)), ap(vw(s, a, n)), ap(t)), [t], [vw(q, a, n), vw(s, a, n)])

    def mm(bank, lq, ls, la, rq, rs, ra, n):
        o = vw("pb%d" % bank, 0, n)
        rd = [vw(lq, la, 128), vw(ls, la, 128), vw(rq, ra, n), vw(rs, ra, n)]
        do("p", lambda: g.tensor.matmul_mx(ap(o), ap(rd[0]), ap(rd[1]), ap(rd[2]), ap(rd[3]), True, True), rd, [o])
        return o

    def send(dst, out, in_, sem, codes=False):
        order("g", "g", [in_], [])
        rid, pid = topo.addr(dst)[:2]
        o, i = (ap(out).bitcast(dt.uint8), ap(in_).bitcast(dt.uint8)) if codes else (ap(out), ap(in_))
        g.remote_dma(o, i, T.sem[sem], T.sem.sent, pid, rid, topo.mask(core, dst))
        total["sent"] = total.get("sent", 0) + len(topo.engines(core, dst))

    nxt = {}

    def place(buf, n):
        a = nxt.get(buf, 0)
        nxt[buf] = a + n
        return a

    def row():
        return place("rows", C)

    def rv(a, lo=0, n=C):
        return vw("rows", a + lo, n)

    def tab():
        return vw("tf", place("tf", KT), KT)

    def off(n=KT):
        return vw("tu", place("tu", n), n)

    def part(o, lo, n):
        return (o[0], o[1] + lo, o[1] + lo + n, 1)

    mask = "mask"

    def scan(out, a, lo, n):
        o = vw("sc", out + lo, n)
        m, x = vw(mask, lo, n), rv(a, lo, n)
        do("v", lambda: g.vector.tensor_tensor_scan(ap(o), ap(m), ap(x), 0.0, A.add, A.max), [m, x], [o])

    def picked(s):
        return vw("sc", s + 15, KT, 16)

    col = {k: vw("cols", i, 1) for i, k in enumerate(("p15", "last", "k", "turn", "half_k", "one_2k"))}

    def table(a, o):
        s = place("sc", C)
        scan(s, a, 0, C)
        ts(o, picked(s), col["turn"], None, A.add)

    dma("s", T.xt0[:, 0:2 * C], T.x[:, 0:2 * C], "dx0", 16, [], [vw("xt0", 0, 2 * C)])
    dma("a", T.ut[:, :], T.u[:, :], "du", 16, [], [vw("ut", 0, 512)])
    dma("s", T.xt0[:, 2 * C:4 * C], T.x[:, 2 * C:4 * C], "dx1", 16, [], [vw("xt0", 2 * C, 2 * C)])
    dma("a", T.lai[:, :], T.la[:, :], "dl", 32, [], [vw("lai", 0, KT)])
    dma("a", T.lbi[:, :], T.lb[:, :], "dl", 32, [], [vw("lbi", 0, KT)])
    wait("s", ("dx0", 16, {}))
    wait("s", ("dx1", 16, {}))
    dma("s", T.wq[:, :].bitcast(dt.uint8), T.wc[:, :], "dw", 32, [], [vw("wq", 0, 512)])
    dma("s", T.wp[:, :], T.ws[:, :], "dw", 32, [], [vw("wp", 0, 512)])
    dma("s", T.vt[:, :], T.v[:, :], "dv", 16, [], [vw("vt", 0, 512)])

    do("v", lambda: g.vector.memset(T.ones[:, :], 1.0), [], [vw("ones", 0, 528)])
    do("g", lambda: g.iota(T.im[:, :], [[1, 16]], 128, -1), [], [vw("im", 0, 16)])
    do("g", lambda: g.iota(T.ip[:, :], [[16, 8]], 0, 0), [], [vw("ip", 0, 8)])
    do("g", lambda: g.iota(T.ik[:, :], [[16, KT]], 0, 0), [], [vw("ik", 0, KT)])
    do("g", lambda: g.affine_select(T.et[:, :], T.ones[:, :], [[-1, 528]], A.is_equal, 0.0, 8, 4), [vw("ones", 0, 528)], [vw("et", 0, 528)])
    ident = row()
    do("g", lambda: g.iota(ap(rv(ident)), [[1, C]], -int(MID), 0, allow_small_or_imprecise_dtypes=True), [], [rv(ident)])
    do("g", lambda: g.iota(T.num[:, :], [[1, C]], 0, 0, allow_small_or_imprecise_dtypes=True), [], [vw("num", 0, C)])
    im2 = vw("im2", 0, 16)
    ts(im2, vw("im", 0, 16), 15, None, A.bitwise_and)
    tcopy(vw("plist", 0, 8), vw("ip", 0, 8))
    ts(vw("ma", 0, 16), im2, 0, -BIG, A.is_equal, A.mult)
    ts(vw("mb", 0, 16), im2, 1, LIFT, A.is_equal, A.mult)
    tt(vw(mask, 0, 16), vw("ma", 0, 16), vw("mb", 0, 16), A.add)
    n = 16
    while n < C:
        m = min(n, C - n)
        tcopy(vw(mask, n, m), vw(mask, 0, m))
        n += m
    z = tab()
    zc = (z[0], z[1], z[1] + 1, 1)
    ts(zc, vw("im2", 0, 1), 0, 16, A.not_equal, A.mult)
    tt(col["p15"], zc, vw("im2", 0, 1), A.subtract)
    ts(col["k"], vw("im2", 0, 1), 1, LIFT, A.not_equal, A.mult)
    ts(col["turn"], col["k"], -1.0, MID, A.mult, A.add)
    ts(col["half_k"], col["k"], 0.5, None, A.add)
    ts(col["one_2k"], col["k"], 2.0, 1.0, A.mult, A.add)
    num_t, low_t = tab(), tab()
    ts(num_t, vw("ik", 0, KT), col["p15"], None, A.add)
    ts(low_t, num_t, -MID, col["k"], A.add, A.add)
    for b in range(4):
        quant("qe", "qes", "et", 128 * b, 128, 8 - b)
    quant("qu", "qus", "ut", 0, 128)
    do("v", lambda: g.vector.tensor_copy(T.qr[:, :].bitcast(dt.uint32), T.qu[:, :].bitcast(dt.uint32).indirect(T.plist[:, 0:8])), [vw("qu", 0, 128), vw("plist", 0, 8)], [vw("qr", 0, 128)])
    do("a", lambda: g.scalar.activation(T.qrs[:, :], T.qus[:, :].indirect(T.plist[:, 0:8]), F.Copy), [vw("qus", 0, 128), vw("plist", 0, 8)], [vw("qrs", 0, 128)])
    act(vw("et8", 0, 528), vw("et", 0, 528), 0.125)
    diff, base = tab(), tab()
    lift = tab()

    S_BANK = (0, 7)
    chg_s = None

    def exchange(diff, base, s):
        sg, d2, dd, e, b2 = tab(), tab(), tab(), tab(), tab()
        return [lambda: ts(sg, picked(s), -2.0, col["one_2k"], A.mult, A.add), lambda: tt(d2, diff, sg, A.mult), lambda: tt(dd, diff, d2, A.subtract),
                lambda: ts(e, dd, col["half_k"], None, A.mult), lambda: tt(b2, base, e, A.add), d2, b2]

    for r, d in enumerate(STEPS):
        last = r == len(STEPS) - 1
        dst = T.cores[(me + d) % n_ranks]
        q, qs, xt = "q%d" % r, "qs%d" % r, "xt%d" % r
        lq, lp, t1l, t2l = "lq%d" % r, "lp%d" % r, "t1l%d" % r, "t2l%d" % r
        src = T.cores[(me - d) % n_ranks]
        ne = len(topo.engines(src, core))
        total["aq%d" % r], total["at%d" % r], total["au%d" % r] = 2 * ne, ne, ne
        note("dma", [], [vw(lq, 0, C), vw(lp, 0, C)], ("aq%d" % r, 2 * ne, {}))
        note("dma", [], [vw(t1l, 0, KT)], ("at%d" % r, ne, {}))
        total["av%d" % r] = ne
        note("dma", [], [vw(t2l, 0, KT)], ("au%d" % r, ne, {}))
        note("dma", [], [vw(t2l, KT, KT)], ("av%d" % r, ne, {}))
        f, zt, h, o = ["%s%d" % (k, r) for k in ("f", "zt", "h", "o")]
        fd, za, zad, zb, zbd, hg = "fd", "za", "zad", "zb", "zbd", "zbd"
        nxt["sc"] = 0

        def plane(t, b, lo=0, n=C):
            return vw(t, C * b + lo, n)

        sv = []
        for i in range(2):
            quant(q, qs, xt, HALF * i, HALF)
            sv.append(mm(S_BANK[i], "qr", "qrs", 0, q, qs, HALF * i, HALF))
        send(dst, vw(lq, 0, C), vw(q, 0, C), "aq%d" % r, True)
        send(dst, vw(lp, 0, C), vw(qs, 0, C), "aq%d" % r)
        neg = row()
        if r == 0:
            tt(diff, vw("lbi", 0, KT), vw("lai", 0, KT), A.subtract)
            for b in range(2):
                quant("qe8", "qe8s", "et8", 128 * b, 128, 6 - b)
            ts(lift, diff, col["k"], None, A.mult)
        if chg_s is not None:
            xs = exchange(diff, base, chg_s)
            for n in range(3):
                xs[n]()
        for i in range(2):
            ts(rv(neg, HALF * i, HALF), sv[i], 0.0, None, A.is_lt)
            if chg_s is not None:
                xs[3 + i]()
            elif i == 0:
                tt(base, vw("lai", 0, KT), lift, A.subtract)
        if chg_s is not None:
            diff, base = xs[5], xs[6]
        s = place("sc", C)
        scan(s, neg, 0, C)
        w, p_t, to_self = tab(), tab(), tab()
        tt(w, picked(s), diff, A.mult)
        tt(p_t, w, base, A.add)
        t_k = off()
        tcopy(t_k, p_t)
        at = row()
        for qq, lo in (("v", 0), ("a", HALF)):
            gather(qq, rv(at, lo, HALF), rv(ident), part(t_k, lo // 16, HALF // 16))
        sf, sr = "sf%d" % r, "sr%d" % r
        own_f = [mm(5 + b, "qe", "qes", 128 * b, q, qs, 0, C) for b in range(2)]

        def copy_own(k):
            b, lo = k // 2, HALF * (k % 2)
            if k == 6:
                act(vw(sf, 0, HALF), sv[0])
            else:
                act(plane(o, b, lo, HALF), part(own_f[b], lo, HALF))
            if k in (1, 3):
                b2 = 2 + k // 2
                own_f.append(mm(3 + b2, "qe", "qes", 128 * b2, q, qs, 0, C))

        tt(to_self, num_t, p_t, A.subtract)

        low, twin = at, row()
        tcopy(rv(twin), rv(at))
        for k in range(7):
            at2, low2, twin2, t2 = row(), row(), row(), off()
            gather("a", rv(at2), rv(at), t_k)
            copy_own(k)
            tt(rv(low2), rv(low), rv(twin), A.min, t_k)
            ss = place("sc", C)
            scan(ss, at2, 0, C)
            tcopy(rv(twin2, 0, TWIN), rv(low2, 0, TWIN))
            ts(t2, picked(ss), col["turn"], None, A.add)
            tcopy(rv(twin2, TWIN, C - TWIN), rv(low2, TWIN, C - TWIN))
            at, low, twin, t_k = at2, low2, twin2, t2
        act(vw(sf, HALF, HALF), sv[1])
        fp = []
        for b in range(4):
            if b < 2:
                fp.append(mm(1 + b, "qe", "qes", 128 * b, lq, lp, 0, C))
                act(plane(f, b), fp[b], 0.125)
            else:
                fp.append(mm(1 + b, "qe8", "qe8s", 128 * (b - 2), lq, lp, 0, C))
                act(plane(f, b), fp[b])
        low2, twin2, m = row(), row(), row()
        tt(rv(low2), rv(low), rv(twin), A.min, t_k)
        tcopy(rv(twin2, 0, 128), rv(low2, 0, 128))
        s = place("sc", C)
        o1, x1 = vw("sc", s + 128, C - 128), rv(low2, 128, C - 128)
        mk = vw(mask, 128, C - 128)
        do("v", lambda: g.vector.tensor_tensor_scan(ap(o1), ap(mk), ap(x1), 0.0, A.add, A.max), [mk, x1], [o1])
        tt(rv(m, 0, 128), rv(low2), rv(twin2, 0, 128), A.min, part(t_k, 0, 8))
        scan(s, m, 0, 128)
        eq, mv, t_f, tears = tab(), tab(), tab(), off()
        tt(eq, picked(s), low_t, A.is_equal)
        tt(mv, eq, to_self, A.mult)
        tt(t_f, mv, p_t, A.add)
        tcopy(tears, t_f)
        send(dst, vw(t1l, 0, KT), tears, "at%d" % r)

        tr, tr2, tr4 = row(), row(), row()
        both = off(2 * KT)
        jump2, jump4 = part(both, 0, KT), part(both, KT, KT)
        for out, win in ((tr, ident), (tr2, tr)):
            for qq, lo in (("v", 0), ("a", HALF)):
                gather(qq, rv(out, lo, HALF), rv(win), part(tears, lo // 16, HALF // 16))
        act(plane(fd, 0), plane(f, 0))
        table(tr2, jump2)
        send(dst, vw(t2l, 0, KT), jump2, "au%d" % r)
        gather("a", rv(tr4), rv(tr2), jump2)
        tcopy(rv(twin2, 128, C - 128), rv(low2, 128, C - 128))
        tt(rv(m, 128, C - 128), rv(low2), rv(twin2, 128, C - 128), A.min, part(t_k, 8, KT - 8))
        table(tr4, jump4)
        send(dst, vw(t2l, KT, KT), jump4, "av%d" % r)
        if r == 0:
            quant("qv", "qvs", "vt", 0, 128)
        act(plane(fd, 1), plane(f, 1))

        lead = [m, row(), row(), row()]
        for b in range(2, 4):
            gather("a", plane(fd, b), plane(f, b), vw(t1l, 0, KT))
        for b in range(4):
            if b < 2:
                tt(plane(za, b), plane(f, b), plane(fd, b), A.add, vw(t1l, 0, KT))
            else:
                tt(plane(za, b), fp[b], plane(fd, b), A.add)
            twin_of(b, plane(zad, b), plane(za, b))
        gather("a", rv(lead[1]), rv(m), t_k)
        act(plane(o, 3, 0, HALF), part(own_f[3], 0, HALF))
        for b in range(4):
            tt(plane(zb, b), plane(za, b), plane(zad, b), A.add, vw(t2l, 0, KT))
            if b == 1:
                gather("a", rv(lead[2]), rv(lead[1]), t_k)
            twin_of(b, plane(zbd, b), plane(zb, b))
        gather("a", rv(lead[3]), rv(lead[2]), t_k)
        for b in range(4):
            tt(vw(zt, b, C, 4), plane(zb, b), plane(zbd, b), A.add, vw(t2l, KT, KT))
            if b == 2:
                t_r = off()
                table(lead[3], t_r)
                for i in range(2):
                    gather("a", vw(sr, HALF * i, HALF), vw(sf, 0, C), part(t_r, HALF * i // 16, HALF // 16))
        zq, zp = "zq%d" % r, "zp%d" % r
        for i in range(2):
            quant(zq, zp, zt, HALF * i, HALF)
            hb = mm((1, 5)[i], "wq", "wp", 0, zq, zp, HALF * i, HALF)
            act(plane(h, 0, HALF * i, HALF), hb, 0.03125)
        for b in range(1, 4):
            hb = mm(1 + b, "wq", "wp", 128 * b, zq, zp, 0, C)
            act(plane(h, b), hb, 0.03125)
        chg = row()
        for i in range(2):
            tt(rv(chg, HALF * i, HALF), sv[i], vw(sr, HALF * i, HALF), A.is_lt)
        chg_s = place("sc", C)
        scan(chg_s, chg, 0, C)

        x2 = "xt%d" % (r + 1)
        if not last:
            gather("a", plane(hg, 3, HALF, HALF), plane(h, 3), part(tears, KT // 2, KT // 2))
            for b in range(3):
                tt(vw(x2, b, C, 4), plane(h, b), plane(o, b), A.add, tears)
            tt(vw(x2, 3, HALF, 4), plane(h, 3), plane(o, 3, 0, HALF), A.add, part(tears, 0, KT // 2))
            tt(vw(x2, 4 * HALF + 3, HALF, 4), part(own_f[3], HALF, HALF), plane(hg, 3, HALF, HALF), A.add)
    q, qs = "q3", "qs3"
    for i in range(2):
        lo = HALF * i
        if i == 0:
            gather("a", plane(hg, 3, HALF, HALF), plane(h, 3), part(tears, KT // 2, KT // 2))
            xs = exchange(diff, base, chg_s)
            d2, b2 = xs[5], xs[6]
            lift, l0, l1, t0, t1 = tab(), tab(), tab(), off(), off()
            steps = xs[:5] + [lambda: ts(lift, d2, col["k"], None, A.mult), lambda: tt(l0, lift, b2, A.add), lambda: tcopy(t0, l0),
                              lambda: tt(l1, l0, d2, A.add), lambda: tcopy(t1, l1)]
        for b in range(4 - i):
            tt(vw(x2, 4 * lo + b, HALF, 4), plane(h, b), plane(o, b, lo, HALF), A.add, part(tears, lo // 16, HALF // 16))
            steps.pop(0)()
        if i == 1:
            for n, t in enumerate((t0, t1)):
                gather("a", vw("lsr", C * n, C), vw("num", 0, C), t)
            tt(vw(x2, 4 * lo + 3, HALF, 4), part(own_f[3], lo, HALF), plane(hg, 3, lo, HALF), A.add)
        quant(q, qs, x2, lo, HALF)
        yb = mm((0, 7)[i], "qv", "qvs", 0, q, qs, lo, HALF)
        qv = vw(q, lo, HALF)
        dma("s", T.oc[:, 4 * lo:4 * lo + 4 * HALF], ap(qv).bitcast(dt.uint8), "out", 0, [qv], [])
        for k in range(4):
            dma("s", T.osc[4 * k:4 * k + 4, lo:lo + HALF], T[qs][32 * k:32 * k + 4, lo:lo + HALF], "out", 0, [vw(qs, lo, HALF)], [])
        yv = vw("yt", lo, HALF)
        if i == 0:
            act(yv, yb)
            for n in range(3):
                steps.pop(0)()
        else:
            ts(yv, yb, 1.0, None, A.mult)
        dma("as"[i], T.y[:, lo:lo + HALF], ap(yv), "out", 0, [yv], [])
    dma("a", T.ls[:, :], T.lsr[0:128:16, :], "out", 0, [vw("lsr", 0, 2 * C)], [])
    for sem in sorted(total):
        if known["g"].get(sem, 0) < total[sem]:
            g.wait_ge(T.sem[sem], total[sem])
